import numpy as np, ml_dtypes
CORES = [24,25,26,27,28,29,30,31]
N = 8
BF = ml_dtypes.bfloat16
def gentries(a):
    return np.ascontiguousarray(a.reshape(8, 16, -1).transpose(0, 2, 1)).reshape(8, -1)
def gtable(e):
    e = np.asarray(e); return np.ascontiguousarray(e.reshape(8, -1, 16).transpose(0, 2, 1)).reshape(128, -1).astype(np.int32)
W, C, RO = 4096, 256, 3
LA, LB, LE, WD = 880, 1040, 960, 32
def parts(rng):
    x = rng.integers(0, 256, (N, 8, 16, W)); a = rng.integers(0, W, (N, 8, C, 16)); p = rng.integers(0, W, (N, 8, C, 16))
    pool = rng.integers(0, W, (N, 8, 32)); hot = np.take_along_axis(pool, rng.integers(0, 32, (N, 8, C * 16)), 2).reshape(N, 8, C, 16)
    return x, a, np.where(rng.random((N, 8, C, 16)) < 0.3, hot, p)
def pack(x, a, p):
    return {"x0": np.ascontiguousarray(x.reshape(N, 128, W)).astype(np.float32).astype(BF), "ka": np.stack([gtable(v.reshape(8, -1)) for v in a]), "ph": np.stack([gtable(v.reshape(8, -1)) for v in p])}
def alike(rng, a, p, share):
    m = (rng.random((N, 8, C, 1)) < share) & (np.arange(16) == rng.integers(0, 16, (N, 8, C, 1)))
    return np.where(m, a, p)
def setup_inputs(rng):
    x, a, p = parts(rng)
    return pack(x, a, alike(rng, a, p, 0.08))
def setup_inputs_spread(rng):
    x, a, p = parts(rng)
    v = np.minimum((np.exp2(8 * rng.random((N, 8, 1, W))) * rng.random(x.shape)).astype(np.int64), 255)
    x = np.where(rng.random(x.shape) < 0.5, v, 255 - v)
    a = np.minimum((W * rng.random(a.shape) ** 2).astype(np.int64), W - 1); u = np.minimum((W * rng.random(a.shape) ** 3).astype(np.int64), W - 1)
    return pack(x, a, np.where(rng.random(a.shape) < 0.5, u, p))
def setup_inputs_ends(rng):
    x, a, p = parts(rng); x = 255 * rng.integers(0, 2, x.shape)
    h = rng.choice(np.array([3, 4, 4, 5, 16]), (N, 8)); h[N - 1, 7] = 16; h[0, 7] = 4; h[0, 0] = 4; h[0, 1] = 3; h[N - 1, 6] = 4
    for r in range(N):
        for g in range(8):
            w = x[r, g]; w[:, W - 1] = w[:, 0]; o = rng.permutation(16)[:h[r, g]]
            if h[r, g] == 16: w[:, 0] = 0
            w[o, W - 1] = 255 - w[o, 0]
    kind = rng.choice(np.array([0, 1, 2]), (N, 8, C, 1), p=[0.4, 0.34, 0.26]); kind[:, :, [0, 1, 3, C - 2, C - 1]] = 0
    e = rng.integers(0, 2, (N, 8, C, 1))
    a = np.where(kind == 0, e * (W - 1), np.where(kind == 1, (W - 1) * rng.integers(0, 2, a.shape), a))
    p = np.where(kind == 0, (1 - e) * (W - 1), np.where(kind == 1, (W - 1) * rng.integers(0, 2, a.shape), p))
    return pack(x, a, p)
def setup_inputs_corners(rng):
    x = np.zeros((N, 8, 16, W), np.int64); a = np.zeros((N, 8, C, 16), np.int64); p = np.zeros((N, 8, C, 16), np.int64)
    far = np.array([LA - 1, LA, LA + 1, LB - 1, LB, LB + 3, LB + 4, LB + 59, LB + 60]); h = W // 2; M = 36; lane = np.arange(16)
    signs = np.stack([np.ones(16, np.int64), -np.ones(16, np.int64), 1 - 2 * (lane & 1)])
    for g in range(8):
        q = rng.permutation(W); low = q[1:h]; high = q[h + M:]; mids = q[h:h + M]
        m0 = rng.choice(np.array([-1, 0, 15, 15, 6]), C); o = lane[None, :] == m0[:, None]; o = o ^ (rng.random((C, 1)) < 0.5)
        k = rng.integers(0, 16, C); k = np.where(k == m0, (k + 1) & 15, k); swap = rng.random(C) < 0.5
        for r in range(N):
            w = x[r, g]; w[:, low] = rng.integers(0, 31, (16, len(low))); w[:, high] = rng.integers(215, 256, (16, len(high)))
            b = rng.integers(100, 151, 16); w[:, q[0]] = b; T = rng.permutation(np.resize(far, M))
            am = T[None, :] // 16 + (lane[:, None] < T[None, :] % 16); w[:, mids] = b[:, None] + am * signs[rng.integers(0, 3, M)].T
            lo1 = low[rng.integers(0, len(low), (C, 16))]; lo2 = low[rng.integers(0, len(low), (C, 16))]; hi1 = high[rng.integers(0, len(high), (C, 16))]; hi2 = high[rng.integers(0, len(high), (C, 16))]
            u = np.where(o, hi1, lo1); v = np.where(o, lo2, hi2)
            n = (0, 16, 15, C, 1, 17, 14, 31)[(g + 3 * r) % 8]; oc = rng.permutation(C); die = oc[:n]; rest = oc[n:]
            v[die, k[die]] = np.where(o[die, k[die]], hi2[die, k[die]], lo2[die, k[die]])
            edge = die[1::2]; under = mids[T == LA - 1]; md = under[rng.integers(0, len(under), len(edge))]
            u[edge, k[edge]] = np.where(swap[edge], md, q[0]); v[edge, k[edge]] = np.where(swap[edge], q[0], md)
            over = mids[T >= LA]; md = over[rng.integers(0, len(over), len(rest))]
            u[rest, k[rest]] = np.where(swap[rest], md, q[0]); v[rest, k[rest]] = np.where(swap[rest], q[0], md)
            assert int(np.sum(np.min(np.add.reduce(np.abs(w[:, u] - w[:, v]), axis=0), axis=1) < LA)) == n
            a[r, g] = u; p[r, g] = v
    return pack(x, a, p)
def setup_inputs_full(rng):
    x, a, p = parts(rng); lane = np.arange(16); h = W // 2; u = W // 4; z = int(rng.integers(0, N)); dead = int(rng.integers(0, 8))
    for g in range(8):
        if g == dead: continue
        for r in range(N):
            w = x[r, g]; q = rng.permutation(W); right = q[:h]; left = q[h:h + u]; out = q[h + u:]; b = rng.integers(100, 151, (16, 1))
            w[:, right] = b + rng.integers(0, 4, (16, h))
            far = np.where(rng.random((16, u)) < 0.5, 78 + rng.integers(0, 3, (16, u)), -75 - rng.integers(0, 3, (16, u)))
            near = np.argsort(rng.random((16, u)), axis=0) < 4
            w[:, left] = b + np.where(near, rng.integers(-8, 12, (16, u)), far)
            w[:, out] = b + rng.integers(90, 100, (16, len(out))) * (1 - 2 * rng.integers(0, 2, (16, len(out))))
            i = (rng.permutation(h)[:C], np.full(C, int(rng.integers(0, h))), rng.integers(0, 6, C))[(g + r) % 3]
            here = lane[None, :] == rng.integers(0, 16, (C, 1))
            a[r, g] = np.where(here, left[rng.integers(0, u, (C, 16))], right[rng.integers(0, h, (C, 16))])
            p[r, g] = np.where(here, right[i][:, None], out[rng.integers(0, len(out), (C, 16))])
    q = rng.permutation(np.arange(1, W)); s1 = q[:h]; s2 = q[h:h + u]; s0 = np.append(q[h + u:], 0)
    a[:, dead] = 0; p[:, dead] = s0[rng.integers(0, len(s0), (N, C, 16))]
    far = np.array([LB - 1, LB, LB + 1, LB + 3, LB + 4, LB + 31, LB + 59, LB + 60]); T = far[np.arange(h) % 8]
    cl = np.minimum(rng.integers(0, 8, (C, 1)) + rng.integers(0, 3, (C, 16)), 7)
    a[(z - 2) % N, dead] = s1[cl + 8 * rng.integers(0, h // 8, (C, 16))]; p[(z + 2) % N, dead] = s2[rng.integers(0, u, (C, 16))]
    x[:, dead] = rng.integers(215, 256, (N, 16, W))
    for r in range(N):
        w = x[r, dead]; w[:, s1] = rng.integers(0, 31, (16, h))
        if r == z:
            b = rng.integers(100, 151, (16, 1)); w[:] = b + rng.integers(0, 4, (16, W)); w[:, s2] = b
            w[:, s1] = b + (T[None, :] // 16 + (lane[:, None] < T[None, :] % 16)) * (1 - 2 * rng.integers(0, 2, (16, h)))
    return pack(x, a, p)
def setup_inputs_ties(rng):
    x, a, p = parts(rng); x = rng.integers(0, 176, x.shape)
    pool = rng.integers(0, W, (N, 8, 8)); pool[..., 0] = 0; pool[..., 7] = W - 1
    hot = np.take_along_axis(pool, rng.integers(0, 8, (N, 8, C * 16)), 2).reshape(N, 8, C, 16); p[:, 1::2] = hot[:, 1::2]
    src = np.arange(16) % rng.choice(np.array([1, 1, 1, 2, 4, 16]), (N, 8, C, 1))
    return pack(x, np.take_along_axis(a, src, 3), np.take_along_axis(p, src, 3))
def check_inputs(d):
    bad = []
    for k, lo, hi in (("x0", 0, 255), ("ka", 0, W - 1), ("ph", 0, W - 1)):
        v = np.asarray(d[k]).astype(np.float64)
        if not (np.min(v) >= lo and np.max(v) <= hi): bad.append("range of " + k)
    v = np.asarray(d["x0"]).astype(np.float64)
    if np.any(v != np.floor(v)): bad.append("whole numbers of x0")
    return bad
def reference(x0, ka, ph):
    X = x0.astype(np.float32).astype(np.int32).reshape(N, 8, 16, W)
    K = np.stack([gentries(v) for v in ka]).astype(np.int64).reshape(N, 8, C, 16)
    P = np.stack([gentries(v) for v in ph]).astype(np.int64).reshape(N, 8, C, 16)
    A = np.zeros((N, 8, 1), np.int64); place = np.arange(16)
    for t in range(RO):
        if t > 0: K = np.roll(K, 1, axis=0); P = np.roll(P, -1, axis=0)
        for r in range(N):
            x, a, p = X[r], K[r].copy(), P[r].copy()
            s = np.take_along_axis(x, a.reshape(8, 1, C * 16), 2).reshape(8, 16, C, 16); y = np.take_along_axis(x, p.reshape(8, 1, C * 16), 2).reshape(8, 16, C, 16)
            D = np.add.reduce(np.abs(s - y), axis=1)
            k = np.argmin(D, axis=2)
            d = np.take_along_axis(D, k[:, :, None], 2)[:, :, 0]
            sk = np.take_along_axis(s, k[:, None, :, None], 3)[..., 0]; yk = np.take_along_axis(y, k[:, None, :, None], 3)[..., 0]
            kill = d < LA; prime = ~kill & (d < LB + 4 * (A[r] & 15))
            step = np.where(np.add.reduce(sk, axis=1) > np.add.reduce(yk, axis=1), 1, -1) * (1 + (d & 3))
            n = np.take_along_axis(p, ((k + step) & 15)[:, :, None], 2)[:, :, 0]
            xn = np.take_along_axis(x, n[:, None, :], 2)
            near = np.add.reduce(np.abs(s - xn[..., None]), axis=1) < LE
            m = np.where(np.any(near, axis=2), np.argmax(near, axis=2), -1)
            fresh = np.take_along_axis(a, np.clip(m[:, :, None] + place, 0, 15), 2); fresh[:, :, 0] = n
            v = np.take_along_axis(p, k[:, :, None], 2)[:, :, 0]; new = np.where(np.abs(sk - yk) <= WD, (yk + 128) & 255, yk)
            for g in range(8):
                c = np.nonzero(prime[g])[0]; w = c[np.unique(v[g, c], return_index=True)[1]]
                x[g][:, v[g, w]] = new[g][:, w]
            P[r] = np.where(kill[:, :, None], (((a * p) >> 5) + p) & (W - 1), p)
            K[r] = np.where(prime[:, :, None], fresh, a)
            A[r] = A[r] + np.add.reduce(kill.astype(np.int64), axis=1)[:, None]
    return {"yk": np.stack([gtable(v.reshape(8, -1)) for v in K]).astype(np.float32), "yp": np.stack([gtable(v.reshape(8, -1)) for v in P]).astype(np.float32), "yx": X.reshape(N, 128, W).astype(np.float32).astype(BF)}

@@ -1,0 +1,494 @@
+from concourse.mybir import AluOpType as ALU, AxisListType, ActivationFunctionType as AF
+
+BIG = 1.0e6
+_B = "bfloat16"
+_F = "float32"
+_I = "int32"
+_U = "uint16"
+SCRATCH = {
+    "X": ("sbuf", [128, 4352], _B),
+    "KS": ("sbuf", [128, 4608], _F),
+    "kd": ("dram", [8, 33, 256], _F),
+    "kz": ("dram", [8, 4096], _F),
+    "cm": ("sbuf", [128, 256], _F),
+    "k15": ("sbuf", [128, 256], _F),
+    "kin": ("sbuf", [128, 256], _I), "pin": ("sbuf", [128, 256], _I),
+    "kl0": ("sbuf", [128, 256], _U), "kl1": ("sbuf", [128, 256], _U), "kl2": ("sbuf", [128, 256], _U),
+    "pl0": ("sbuf", [128, 256], _U), "pl1": ("sbuf", [128, 256], _U), "pl2": ("sbuf", [128, 256], _U),
+    "ku": ("sbuf", [128, 4, 16, 4], _U), "pu": ("sbuf", [128, 256], _U),
+    "kout": ("sbuf", [128, 4, 16, 4], _F), "pout": ("sbuf", [128, 256], _F),
+    "Pf": ("sbuf", [128, 256], _F), "P4": ("sbuf", [128, 256], _F),
+    "t1": ("sbuf", [128, 256], _I), "t2": ("sbuf", [128, 256], _I),
+    "pw": ("sbuf", [128, 256], _I), "px_": ("sbuf", [128, 256], _I),
+    "pid": ("sbuf", [128, 4], _I), "row": ("sbuf", [128, 128], _I), "row2": ("sbuf", [128, 128], _I),
+    "rowm": ("sbuf", [128, 128], _F), "rowi": ("sbuf", [128, 128], _F),
+    "col": ("sbuf", [128, 16], _F), "r16": ("sbuf", [128, 16], _F), "OH": ("sbuf", [128, 16], _F),
+    "GM": ("sbuf", [128, 8], _F), "pw2": ("sbuf", [128, 64], _F),
+    "SEL": ("sbuf", [128, 16, 128], _B), "SELN": ("sbuf", [128, 16, 128], _B),
+    "SELP": ("sbuf", [128, 16, 128], _B), "IDN": ("sbuf", [128, 128], _B),
+    "SELW": ("sbuf", [128, 16, 128], _B), "SELT": ("sbuf", [128, 16, 128], _B),
+    "BLK": ("sbuf", [128, 128], _B), "BLKF": ("sbuf", [128, 128], _F), "BLK0": ("sbuf", [128, 128], _F),
+    "S15": ("sbuf", [128, 128], _F), "ID": ("sbuf", [128, 128], _B), "IDW": ("sbuf", [128, 128], _B),
+    "JR": ("sbuf", [128, 256], _B), "JRF": ("sbuf", [128, 256], _F), "Z0": ("sbuf", [128, 256], _B),
+    "RST": ("sbuf", [128, 256], _F), "RSE": ("sbuf", [128, 256], _F), "BC0": ("sbuf", [128, 256], _F),
+    "C16": ("sbuf", [128, 16], _F), "CB": ("sbuf", [128, 16], _F), "DM": ("sbuf", [128, 16], _F),
+    "DMH": ("sbuf", [128, 16], _F), "TRB": ("sbuf", [128, 4, 64], _B), "tri": ("sbuf", [128, 64], _F),
+    "us": ("sbuf", [128, 256], _F), "key": ("sbuf", [128, 256], _F), "R": ("sbuf", [128, 256], _F), "sg": ("sbuf", [128, 256], _B),
+    "sf": ("sbuf", [128, 384], _F), "si": ("sbuf", [128, 128], _I),
+    "offF": ("sbuf", [128, 16], _U), "offK": ("sbuf", [128, 16], _U), "offV": ("sbuf", [128, 16], _U),
+    "offX": ("sbuf", [128, 16], _U),
+    "kill": ("sbuf", [128, 16], _B), "k1b": ("sbuf", [128, 16], _B), "f1b": ("sbuf", [128, 16], _B),
+    "A": ("sbuf", [128, 4], _F), "A1": ("sbuf", [128, 4], _F), "Ai": ("sbuf", [128, 4], _I), "thr": ("sbuf", [128, 4], _F),
+    "xn": ("sbuf", [128, 4, 64], _B), "xz": ("sbuf", [128, 256], _F), "xb": ("sbuf", [128, 256], _F),
+    "nn": ("sbuf", [128, 256], _F), "fs": ("sbuf", [128, 256], _F), "a1": ("sbuf", [128, 256], _F),
+    "kp": ("sbuf", [128, 4, 64], _F),
+    "HPk": ("sbuf", [128, 4, 16, 4], _F), "HPf": ("sbuf", [128, 4, 16, 4], _F),
+    "b1": ("sbuf", [128, 256], _I), "b2": ("sbuf", [128, 256], _I), "FB": ("sbuf", [128, 256], _B),
+    "BD": ("sbuf", [128, 16, 8, 16], _B), "junk": ("sbuf", [128, 4096], _B),
+    "ak": ("sbuf", [128, 256], _B), "yk_": ("sbuf", [128, 256], _B), "sw": ("sbuf", [128, 256], _B),
+    "sy": ("sbuf", [128, 256], _B), "e2": ("sbuf", [128, 256], _B),
+    "pk": ("psum", [128, 512], _F), "ps": ("psum", [128, 512], _F), "px": ("psum", [128, 4, 16, 4], _F),
+    "pe": ("psum", [128, 256], _F), "pb": ("psum", [128, 8, 16, 4], _F), "pone": ("psum", [128, 512], _F),
+    "pn": ("psum", [128, 8, 4, 16], _F), "pg": ("psum", [128, 512], _F),
+}
+for _c in range(4):
+    for _n in ("y", "s", "d", "rl", "mx"):
+        SCRATCH["%s%d" % (_n, _c)] = ("sbuf", [128, 1024], _B)
+PSUM = ("pk", "ps", "px", "pe", "pb", "pone", "pn", "pg")
+SEMAPHORES = ["qv", "qs", "qt", "qg"] + ["dm%d" % i for i in range(24)] + ["rk1", "rk2", "rp1", "rp2", "lk1", "lk2", "lp1", "lp2"]
+ROUNDS = 3
+SMF = ("w", "h1", "h2", "fo", "ko", "plt", "nk", "pr", "k1", "f1", "pr4", "bs", "bs2", "o1", "o2", "cnt", "nd", "win", "w1", "w2", "w3")
+SMI = ("ki", "zm", "ub", "kk", "h3", "fi")
+
+
+def rank_program(g, core, T, topo):
+    rank = T.rank_of(core)
+    if rank is None:
+        return
+    n_ranks = len(T.cores)
+    eng = {"v": g.vector, "s": g.scalar, "t": g.tensor, "g": g, "y": g.sync}
+    count = {"v": 0, "s": 0, "t": 0, "g": 0}
+    total = {}
+    waited = {}
+    log = {}
+    dmas = [0]
+
+    def deps(q, reads, writes):
+        need = {}
+        for is_w, regs in ((False, reads), (True, writes)):
+            for name, lo, hi in regs:
+                bank = name in PSUM
+                for (l, h, oq, sem, val, ow) in log.get(name, []):
+                    if not bank and (h <= lo or hi <= l):
+                        continue
+                    if oq == q:
+                        if q == "t" or (not ow):
+                            continue
+                        if is_w and bank and (h <= lo or hi <= l):
+                            continue
+                        if not is_w and (h <= lo or hi <= l):
+                            continue
+                    elif not bank and not ow and not is_w:
+                        continue
+                    if val > need.get(sem, 0):
+                        need[sem] = val
+        for sem in sorted(need):
+            if waited.get((q, sem), 0) < need[sem]:
+                waited[(q, sem)] = need[sem]
+                eng[q].wait_ge(T.sem[sem], need[sem])
+
+    def note(q, sem, val, reads, writes):
+        for is_w, regs in ((False, reads), (True, writes)):
+            for name, lo, hi in regs:
+                old = log.get(name, [])
+                if is_w:
+                    old = [e for e in old if not (lo <= e[0] and e[1] <= hi)]
+                else:
+                    old = [e for e in old if not (e[2] == q and not e[5] and e[3] == sem and lo <= e[0] and e[1] <= hi)]
+                old.append((lo, hi, q, sem, val, is_w))
+                log[name] = old
+
+    def m(name):
+        if name in SMF:
+            i = 16 * SMF.index(name)
+            return T.sf[:, i:i + 16]
+        if name in SMI:
+            i = 16 * SMI.index(name)
+            return T.si[:, i:i + 16]
+        return T[name][:]
+
+    def flat(name, lo=None, hi=None):
+        if lo is None and (name in SMF or name in SMI):
+            return (name, 0, 16)
+        if lo is None:
+            n = 1
+            for x in SCRATCH[name][1][1:]:
+                n *= x
+            return (name, 0, n)
+        return (name, lo, hi)
+
+    def op(q, fn, reads, writes):
+        reads = [flat(*r) if isinstance(r, tuple) else flat(r) for r in reads]
+        writes = [flat(*r) if isinstance(r, tuple) else flat(r) for r in writes]
+        deps(q, reads, writes)
+        count[q] += 1
+        sem = "q" + q
+        total[sem] = count[q]
+        fn().then_inc(T.sem[sem], 1)
+        note(q, sem, count[q], reads, writes)
+
+    def dma(q, pairs):
+        sem = "dm%d" % dmas[0]
+        dmas[0] += 1
+        val = 16 * len(pairs)
+        total[sem] = val
+        done = []
+        for out, in_, w, r in pairs:
+            r = [flat(*x) if isinstance(x, tuple) else flat(x) for x in r]
+            w = [flat(*x) if isinstance(x, tuple) else flat(x) for x in w]
+            deps(q, r, w)
+            eng[q].dma_start(out, in_).then_inc(T.sem[sem], 16)
+            done.append((r, w))
+        for r, w in done:
+            note("dma", sem, val, r, [])
+        for r, w in done:
+            for x in w:
+                log.setdefault(x[0], []).append((x[1], x[2], "dma", sem, val, True))
+
+    def tt(out, a, b, o, reads, writes):
+        op("v", lambda: g.vector.tensor_tensor(out, a, b, o), reads, writes)
+
+    def ts(out, a, s1, o1, reads, writes, s2=None, o2=None):
+        if o2 is None:
+            op("v", lambda: g.vector.tensor_scalar(out, a, s1, None, o1), reads, writes)
+        else:
+            op("v", lambda: g.vector.tensor_scalar(out, a, s1, s2, o1, o2), reads, writes)
+
+    def q1(out, a, s1, o1, s2=None, o2=None):
+        ts(m(out), m(a), s1, o1, [a], [out], s2, o2)
+
+    def q2(out, a, b, o):
+        tt(m(out), m(a), m(b), o, [a, b], [out])
+
+    def cp(out, a, reads, writes):
+        op("v", lambda: g.vector.tensor_copy(out, a), reads, writes)
+
+    def fill(name, c, ap=None):
+        op("v", lambda: g.vector.memset(T[name][:] if ap is None else ap, c), [], [name])
+
+    def act(out, a, f, reads, writes, **kw):
+        op("s", lambda: g.scalar.activation(out, a, f, **kw), reads, writes)
+
+    def mm(out, l, r, st, sp, reads, writes):
+        op("t", lambda: g.tensor.matmul(out, l, r, st, sp), reads, writes)
+
+    def scan(out, a, b, o1, o2, reads, writes):
+        op("v", lambda: g.vector.tensor_tensor_scan(out, a, b, 0.0, o1, o2), reads, writes)
+
+    def iota(name, ap, pat, base, mult):
+        op("g", lambda: g.iota(ap, pat, base, mult, allow_small_or_imprecise_dtypes=True), [], [name])
+
+    dma("y", [(T.pin[:], T.ph[:], ["pin"], [])])
+    dma("y", [(T.kin[:], T.ka[:], ["kin"], [])])
+    dma("y", [(T.X[:, 0:4096], T.x0[:], [("X", 0, 4096)], [])])
+    iota("pid", T.pid[:, 0:1], [[0, 1]], 0, 1)
+    iota("row", T.row[:], [[1, 128]], 0, 0)
+    iota("r16", T.r16[:], [[1, 16]], 0, 0)
+    iota("JRF", T.JRF[:], [[0, 16], [4, 16]], 1, 0)
+    iota("C16", T.C16[:], [[0, 4], [16, 4]], 0, 0)
+    iota("CB", T.CB[:], [[64, 4], [1, 4]], 0, 0)
+    iota("DM", T.DM[:], [[16, 16]], 4096, 0)
+    iota("tri", T.tri[:], [[1, 4], [4, 16]], 0, 0)
+    fill("cm", -4096.0)
+    dma("y", [(T.kz[:], T.cm[:], ["kz"], ["cm"]), (T.kd[:, 0, :], T.cm[0:8, :], [("kd", 0, 1)], ["cm"])])
+    dma("y", [(T.KS[0::16, 0:4096], T.kz[:], [("KS", 0, 4096)], ["kz"])])
+    fill("SEL", 0.0)
+    ts(T.pid[:, 1:2], T.pid[:, 0:1], 15, ALU.bitwise_and, [("pid", 0, 1)], [("pid", 1, 2)])
+    ts(T.pid[:, 2:3], T.pid[:, 0:1], 4, ALU.arith_shift_right, [("pid", 0, 1)], [("pid", 2, 3)])
+    ts(T.row2[:], T.row[:], 4, ALU.arith_shift_right, ["row"], ["row2"])
+    cp(T.rowi[:], T.row[:], ["row"], ["rowi"])
+    cp(T.col[:, 0:3], T.pid[:, 0:3], [("pid", 0, 3)], [("col", 0, 3)])
+    cp(T.rowm[:], T.row2[:], ["row2"], ["rowm"])
+    ts(T.col[:, 3:4], T.col[:, 1:2], 1.0, ALU.add, [("col", 1, 2)], [("col", 3, 4)])
+    ts(T.col[:, 4:5], T.col[:, 1:2], 64.0, ALU.mult, [("col", 1, 2)], [("col", 4, 5)])
+    ts(T.col[:, 7:8], T.col[:, 1:2], 4.0, ALU.mult, [("col", 1, 2)], [("col", 7, 8)])
+    ts(T.BLK[:], T.rowm[:], T.col[:, 2:3], ALU.is_equal, ["rowm", ("col", 2, 3)], ["BLK"])
+    ts(T.OH[:], T.r16[:], T.col[:, 1:2], ALU.is_equal, ["r16", ("col", 1, 2)], ["OH"])
+    for q in range(16):
+        cp(T.SEL[:, q, q::16], T.BLK[:, q::16], ["BLK"], [("SEL", 128 * q, 128 * q + 128)])
+    act(T.SELN[:], T.SEL[:], AF.Copy, ["SEL"], ["SELN"], scale=-0.5)
+    ts(T.ID[:], T.rowi[:], T.col[:, 0:1], ALU.is_equal, ["rowi", ("col", 0, 1)], ["ID"])
+    ts(T.IDW[:], T.ID[:], 1.0 / 128, ALU.mult, ["ID"], ["IDW"])
+    ts(T.IDN[:], T.ID[:], -1.0, ALU.mult, ["ID"], ["IDN"])
+    ts(T.JR[:], T.JRF[:], 1.0 / 128, ALU.mult, ["JRF"], ["JR"])
+    cp(T.kl0[:], T.kin[:], ["kin"], ["kl0"])
+    cp(T.pl0[:], T.pin[:], ["pin"], ["pl0"])
+    fill("RST", -BIG)
+    op("v", lambda: g.vector.memset(T.RST[:, 0::16], BIG), ["RST"], ["RST"])
+    fill("thr", 520.0)
+    fill("A", 0.0)
+    ts(T.C16[:], T.C16[:], T.col[:, 4:5], ALU.add, ["C16", ("col", 4, 5)], ["C16"])
+    ts(T.CB[:], T.CB[:], T.col[:, 7:8], ALU.add, ["CB", ("col", 7, 8)], ["CB"])
+    ts(T.DM[:], T.DM[:], T.col[:, 1:2], ALU.add, ["DM", ("col", 1, 2)], ["DM"])
+    ts(T.DMH[:], T.DM[:], -2047.5, ALU.add, ["DM"], ["DMH"])
+
+    def constants2():
+        for q in range(16):
+            ts(T.SELT[:, q, :], T.BLK[:], T.OH[:, q:q + 1], ALU.mult, ["BLK", "OH"], [("SELT", 128 * q, 128 * q + 128)])
+        cp(T.BLKF[:], T.BLK[:], ["BLK"], ["BLKF"])
+        fill("BLK0", 0.0)
+        op("v", lambda: g.vector.tensor_copy(T.BLK0[:, 0::16], T.BLK[:, 0::16]), ["BLK", "BLK0"], ["BLK0"])
+        ts(T.S15[:], T.BLK[:], T.OH[:, 15:16], ALU.mult, ["BLK", "OH"], ["S15"])
+        fill("Z0", 0.0)
+        fill("RSE", -1.0 / 16)
+        op("v", lambda: g.vector.memset(T.RSE[:, 0::16], BIG), ["RSE"], ["RSE"])
+        fill("BC0", 1.0)
+        op("v", lambda: g.vector.memset(T.BC0[:, 0::16], 0.0), ["BC0"], ["BC0"])
+        fill("xz", 0.0)
+        ts(T.GM[:], T.r16[:, 0:8], T.col[:, 2:3], ALU.is_equal, ["r16", ("col", 2, 3)], ["GM"])
+        fill("pw2", 0.5, T.pw2[:, 0:16])
+        fill("pw2", 2.0, T.pw2[:, 16:32])
+        op("v", lambda: g.vector.tensor_tensor_scan(T.pw2[:, 32:48], T.pw2[:, 0:16], T.Z0[:, 0:16], 8192.0, ALU.mult, ALU.add), ["pw2", "Z0"], ["pw2"])
+        op("v", lambda: g.vector.tensor_tensor_scan(T.pw2[:, 48:64], T.pw2[:, 16:32], T.Z0[:, 0:16], 0.25, ALU.mult, ALU.add), ["pw2", "Z0"], ["pw2"])
+        op("v", lambda: g.vector.memset(T.pw2[:, 45:48], 0.0), ["pw2"], ["pw2"])
+        op("v", lambda: g.vector.memset(T.pw2[:, 60:64], 0.0), ["pw2"], ["pw2"])
+        for i in (0, 1):
+            a = 32 + 16 * i
+            tt(T.pw2[:, 16 * i:16 * i + 16], T.pw2[:, a:a + 16], T.OH[:], ALU.mult, ["pw2", "OH"], ["pw2"])
+            op("v", lambda i=i: g.vector.tensor_reduce(T.col[:, 5 + i:6 + i], T.pw2[:, 16 * i:16 * i + 16], AxisListType.X, ALU.add), ["pw2"], [("col", 5 + i, 6 + i)])
+        act(T.SELW[:], T.SEL[:], AF.Copy, ["SEL", ("col", 6, 7)], ["SELW"], scale=T.col[:, 6:7])
+        act(T.SELP[:], T.SEL[:], AF.Copy, ["SEL"], ["SELP"], scale=0.5)
+        for rl in range(4):
+            ts(T.col[:, 8 + rl:9 + rl], T.col[:, 7:8], float(rl), ALU.add, [("col", 7, 8)], [("col", 8 + rl, 9 + rl)])
+        for rl in range(4):
+            ts(T.TRB[:, rl, :], T.tri[:], T.col[:, 8 + rl:9 + rl], ALU.is_ge, ["tri", ("col", 8 + rl, 9 + rl)], [("TRB", 64 * rl, 64 * rl + 64)], -64.0, ALU.mult)
+
+    def landed(name, sem, val):
+        total[sem] = val
+        log.setdefault(name, []).append((0, 256, "rem", sem, val, True))
+
+    def send(name, land, dst, rs, ls):
+        rid, pid, _ = topo.addr(dst)
+        es = topo.engines(core, dst)[:8]
+        mask = sum(1 << e for e in es)
+        regs = [flat(name)]
+        deps("g", regs, [])
+        g.remote_dma(T[land][:], T[name][:], T.sem[rs], T.sem[ls], pid, rid, mask)
+        total[ls] = len(es)
+        note("rem", ls, len(es), regs, [])
+
+    nxt = T.cores[(rank + 1) % n_ranks]
+    prv = T.cores[(rank - 1) % n_ranks]
+    KB = 17 * 256
+    CN = 16 * SMF.index("cnt")
+
+    for t in range(ROUNDS):
+        last = t == ROUNDS - 1
+        kl, pl = "kl%d" % t, "pl%d" % t
+        KL, PL = T[kl], T[pl]
+        if t:
+            ne = len(topo.engines(core, nxt)[:8])
+            landed(kl, "rk%d" % t, ne)
+            landed(pl, "rp%d" % t, ne)
+        if t == 0:
+            fill("us", 0.0)
+            constants2()
+        cp(T.y0[:], T.X[:, 0:4096].indirect(PL[:, 0:64]), [("X", 0, 4096), pl], ["y0"])
+        for c in (1, 2, 3):
+            act(T["y%d" % c][:], T.X[:, 0:4096].indirect(PL[:, 64 * c:64 * c + 64]), AF.Copy, [("X", 0, 4096), pl], ["y%d" % c])
+        cp(T.Pf[:], PL[:], [pl], ["Pf"])
+        ts(T.P4[:], PL[:], 4096.0, ALU.add, [pl], ["P4"])
+        cp(T.KS[:, KB:KB + 256], KL[:], [kl], [("KS", KB, KB + 256)])
+        mm(T.pn[:, 0:4], T.S15[:], T.KS[:, KB:KB + 256], True, True, ["S15", ("KS", KB, KB + 256)], [("pn", 0, 256)])
+        act(T["s3"][:], T.X[:, 0:4096].indirect(KL[:, 192:256]), AF.Copy, [("X", 0, 4096), kl], ["s3"])
+        act(T.k15[:], T.pn[:, 0:4], AF.Copy, [("pn", 0, 256)], ["k15"])
+        dma("y", [(T.kd[:, 1:17, :], T.KS[:, KB:KB + 256], [("kd", 1, 17)], [("KS", KB, KB + 256)]),
+                  (T.kd[:, 17:33, :], T.k15[:], [("kd", 17, 33)], ["k15"])])
+        dma("y", [(T.KS[j::16, 0:4096], T.kd[:, j + 1:j + 17, :], [("KS", 0, 4096)], [("kd", j + 1, j + 17)]) for j in range(1, 16)]
+            + [(T.KS[:, 4096:KB], T.kd[:, 0:16, :], [("KS", 4096, KB)], [("kd", 0, 16)])])
+        mm(T.pk[:, 0:256], T.ID[:], T.JR[:], True, False, ["ID", "JR"], [("pk", 0, 256)])
+
+        def fused(c):
+            tt(T["d%d" % c][:], T.X[:, 0:4096].indirect(KL[:, 64 * c:64 * c + 64]), T["y%d" % c][:], ALU.subtract, [("X", 0, 4096), kl, "y%d" % c], ["d%d" % c])
+
+        def relu(c):
+            ts(T["rl%d" % c][:], T["d%d" % c][:], 0.0, ALU.max, ["d%d" % c], ["rl%d" % c])
+
+        def pass_(bank, lo, sel, src, first, final, rev=False):
+            for q in range(16):
+                mm(T[bank][:, lo:lo + 64], T[sel][:, q, :], T[src][:, 64 * q:64 * q + 64], first and q == 0, final and q == 15,
+                   [sel, src], [(bank, lo, lo + 64)])
+
+        def dpass(c):
+            pass_("ps", 64 * c, "SELN", "d%d" % c, True, True)
+
+        def rpass(c):
+            pass_("pk", 64 * c, "SEL", "rl%d" % c, False, False)
+
+        def sgather(c):
+            act(T["s%d" % c][:], T.X[:, 0:4096].indirect(KL[:, 64 * c:64 * c + 64]), AF.Copy, [("X", 0, 4096), kl], ["s%d" % c])
+
+        for h, bank in ((0, "pone"), (1, "pg")):
+            mm(T[bank][:], T.ID[:], T.s3[:, 512 * h:512 * h + 512], True, False, ["ID", "s3"], [bank])
+            mm(T[bank][:], T.IDN[:], T.y3[:, 512 * h:512 * h + 512], False, True, ["IDN", "y3"], [bank])
+            act(T.rl3[:, 512 * h:512 * h + 512], T[bank][:], AF.Abs, [bank], [("rl3", 512 * h, 512 * h + 512)], scale=0.5)
+        sgather(0)
+        fused(0)
+        relu(0)
+        fused(1)
+        dpass(0)
+        rpass(0)
+        pass_("ps", 192, "SELN", "s3", True, False)
+        pass_("ps", 192, "SELP", "y3", False, True)
+        rpass(3)
+        relu(1)
+        fused(2)
+        dpass(1)
+        rpass(1)
+        relu(2)
+        dpass(2)
+        rpass(2)
+        tt(T.t1[:], T.KS[:, KB:KB + 256], T.Pf[:], ALU.mult, [("KS", KB, KB + 256), "Pf"], ["t1"])
+        ts(T.t2[:], T.t1[:], 5, ALU.arith_shift_right, ["t1"], ["t2"])
+        sgather(1)
+        act(T.sg[:], T.ps[:, 0:256], AF.Sign, [("ps", 0, 256)], ["sg"], scale=-1.0, bias=-0.25)
+        act(T.us[:, 0:192], T.ps[:, 0:192], AF.Copy, [("ps", 0, 192)], [("us", 0, 192)])
+        mm(T.pk[:, 0:256], T.IDW[:], T.sg[:], False, True, ["IDW", "sg"], [("pk", 0, 256)])
+        sgather(2)
+        tt(T.key[:], T.pk[:, 0:256], T.us[:], ALU.add, [("pk", 0, 256), "us"], ["key"])
+        scan(T.R[:], T.RST[:], T.key[:], ALU.max, ALU.min, ["RST", "key"], ["R"])
+        r = T.R[:, 15::16]
+        ts(m("ki"), r, 64.0, ALU.mult, ["R"], ["ki"])
+        ts(m("nk"), r, 440.0, ALU.is_ge, ["R"], ["nk"])
+        ts(m("plt"), r, T.thr[:, 0:1], ALU.is_lt, ["R", "thr"], ["plt"])
+        q1("ub", "ki", 1, ALU.bitwise_and)
+        q1("zm", "ki", 5, ALU.arith_shift_right, 3, ALU.bitwise_and)
+        q1("kk", "ki", 1, ALU.arith_shift_right, 15, ALU.bitwise_and)
+        q1("w", "ub", 2.0, ALU.mult, -1.0, ALU.add)
+        q2("pr", "plt", "nk", ALU.mult)
+        q2("h2", "zm", "w", ALU.mult)
+        q2("h1", "kk", "w", ALU.add)
+        q2("h3", "h1", "h2", ALU.add)
+        q1("fi", "h3", 15, ALU.bitwise_and)
+        q2("fo", "fi", "C16", ALU.add)
+        cp(T.offF[:], m("fo"), ["fo"], ["offF"])
+        for c in range(4):
+            cp(T.xn[:, c, :], T["y%d" % c][:].indirect(T.offF[:, 4 * c:4 * c + 4]), ["y%d" % c, "offF"], [("xn", 64 * c, 64 * c + 64)])
+        for rl in range(4):
+            mm(T.px[:, :, :, rl], T.ID[:], T.xn[:, :, 16 * rl:16 * rl + 16], True, True, ["ID", "xn"], ["px"])
+        q1("k1", "kk", 1.0, ALU.add)
+        q1("f1", "fi", 1.0, ALU.add)
+        q2("ko", "kk", "C16", ALU.add)
+        q2("k1b", "k1", "pr", ALU.mult)
+        q2("f1b", "f1", "pr", ALU.mult)
+        cp(T.offK[:], m("ko"), ["ko"], ["offK"])
+        ts(T.kill[:], r, 440.0, ALU.is_lt, ["R"], ["kill"])
+
+        def spread(b, src):
+            for q in range(16):
+                mm(T.pb[:, b:b + 4, q, :], T.SELT[:, q, :], T[src][:], True, True, ["SELT", src], [("pb", 64 * b, 64 * b + 256)])
+
+        spread(0, "k1b")
+        spread(4, "f1b")
+        mm(T.pe[:], T.ID[:], T.Z0[:], True, False, ["ID", "Z0"], ["pe"])
+
+        def second(c):
+            pass_("pe", 64 * c, "SELN", "s%d" % c, False, False)
+            for m in range(16):
+                tt(T["mx%d" % c][:, m::16], T["s%d" % c][:, m::16], T.px[:, c], ALU.max, ["s%d" % c, "px"], [("mx%d" % c, 64 * m, 64 * m + 64)])
+            pass_("pe", 64 * c, "SEL", "mx%d" % c, False, c == 3)
+
+        second(0)
+        ts(T.pone[:], T.pb[:], T.col[:, 3:4], ALU.is_equal, ["pb", ("col", 3, 4)], ["pone"])
+        tt(T.HPk[:], T.pone[:, 0:256], T.P4[:], ALU.mult, [("pone", 0, 256), "P4"], ["HPk"])
+        tt(T.HPf[:], T.pone[:, 256:512], T.P4[:], ALU.mult, [("pone", 256, 512), "P4"], ["HPf"])
+        for rl in range(4):
+            mm(T.pn[:, 0:4, rl, :], T.BLKF[:], T.HPk[:, :, :, rl], True, True, ["BLKF", "HPk"], [("pn", 0, 256)])
+        for q in range(16):
+            mm(T.ps[:, 256:272], T.SELN[:, q, :], T.xn[:, :, q::16], q == 0, q == 15, ["SELN", "xn"], [("ps", 256, 272)])
+        spread(0, "kill")
+        for c in range(4):
+            src = "d%d" % c if c < 3 else "rl3"
+            act(T.ak[:, 64 * c:64 * c + 64], T[src][:].indirect(T.offK[:, 4 * c:4 * c + 4]), AF.Abs, [src, "offK"], [("ak", 64 * c, 64 * c + 64)],
+                scale=1.0 if c < 3 else 2.0)
+        for c in range(4):
+            act(T.yk_[:, 64 * c:64 * c + 64], T["y%d" % c][:].indirect(T.offK[:, 4 * c:4 * c + 4]), AF.Copy, ["y%d" % c, "offK"], [("yk_", 64 * c, 64 * c + 64)])
+        act(T.sw[:], T.ak[:], AF.Sign, ["ak"], ["sw"], scale=-1.0, bias=32.5)
+        act(T.sy[:], T.yk_[:], AF.Sign, ["yk_"], ["sy"], scale=-1.0, bias=127.5)
+        second(1)
+        ts(T.b1[:], T.pn[:, 0:4], T.col[:, 5:6], ALU.mult, [("pn", 0, 256), ("col", 5, 6)], ["b1"])
+        ts(T.b2[:], T.b1[:], 4096, ALU.bitwise_and, ["b1"], ["b2"])
+        ts(T.FB[:], T.b2[:], 1.0 / 2048, ALU.mult, ["b2"], ["FB"], -1.0, ALU.add)
+        for i in range(8):
+            ts(T.BD[:, :, i, :], T.FB[:], T.GM[:, i:i + 1], ALU.mult, ["FB", "GM"], [("BD", 256 * i, 256 * i + 256)])
+        for rl in range(4):
+            mm(T.pn[:, 4:8, rl, :], T.BLK0[:], T.HPf[:, :, :, rl], True, True, ["BLK0", "HPf"], [("pn", 256, 512)])
+        act(T.a1[:], T.pn[:, 4:8], AF.Copy, [("pn", 256, 512)], ["a1"])
+        for q in range(16):
+            mm(T.ps[:, 272:288], T.SELW[:, q, :], T.FB[:, q::16], q == 0, q == 15, ["SELW", "FB"], [("ps", 272, 288)])
+        mm(T.ps[:, 288:304], T.BLK[:], T.kill[:], True, True, ["BLK", "kill"], [("ps", 288, 304)])
+        tt(T.pb[:, 4:8], T.t2[:], T.pb[:, 0:4], ALU.mult, ["t2", ("pb", 0, 256)], [("pb", 256, 512)])
+        tt(T.pw[:], T.pb[:, 4:8], T.Pf[:], ALU.add, [("pb", 256, 512), "Pf"], ["pw"])
+        ts(T.px_[:], T.pw[:], 4095, ALU.bitwise_and, ["pw"], ["px_"])
+        if last:
+            cp(T.pout[:], T.px_[:], ["px_"], ["pout"])
+            dma("y", [(T.yp[:], T.pout[:], [], ["pout"])])
+        else:
+            cp(T.pu[:], T.px_[:], ["px_"], ["pu"])
+            send("pu", "pl%d" % (t + 1), prv, "rp%d" % (t + 1), "lp%d" % (t + 1))
+        for bank, rrs in (("pg", (12, 13)), ("pk", (14, 15)), ("pone", (8, 9)), ("pb", (10, 11)), ("pg", (4, 5, 6, 7)), ("pk", (0, 1, 2, 3))):
+            lo = 0
+            todo = []
+            for rr in rrs:
+                rh, rl = rr // 4, rr % 4
+                n = 64 * (rh + 1)
+                G = T[bank][:, lo // 64:(lo + n) // 64] if bank == "pb" else T[bank][:, lo:lo + n]
+                mm(G, T.BD[:, rr, :, :], T.FB[:, 0:n], True, False, ["BD", "FB"], [(bank, lo, lo + n)])
+                G2 = T[bank][:, (lo + n) // 64 - 1:(lo + n) // 64] if bank == "pb" else T[bank][:, lo + n - 64:lo + n]
+                mm(G2, T.ID[:], T.TRB[:, rl, :], False, True, ["ID", "TRB"], [(bank, lo, lo + n)])
+                todo.append((rr, n, lo, G))
+                lo += n
+            for rr, n, lo, G in todo:
+                act(T.junk[:, 256 * rr:256 * rr + n], G, AF.Relu, [(bank, lo, lo + n)], [("cnt", rr, rr + 1), ("junk", 256 * rr, 256 * rr + n)], bias=-15.0,
+                    accum_out=T.sf[:, CN + rr:CN + rr + 1])
+        ts(T.xz[:, 0::16], T.ps[:, 256:272], -1.0, ALU.mult, [("ps", 256, 272)], ["xz"], 480.0, ALU.add)
+        q1("pr4", "pr", 4096.0, ALU.mult)
+        q1("bs", "pr", -512.0, ALU.mult, 4352.0, ALU.add)
+        scan(T.xb[:], T.BC0[:], T.xz[:], ALU.mult, ALU.add, ["BC0", "xz"], ["xb"])
+        q2("bs2", "bs", "CB", ALU.add)
+        second(2)
+        second(3)
+        ts(T.pn[:, 0:4], T.sw[:], 1.0, ALU.add, ["sw"], [("pn", 0, 256)], 64.0, ALU.mult)
+        tt(m("w1"), T.ps[:, 272:288], T.DMH[:], ALU.subtract, [("ps", 272, 288), "DMH"], ["w1"])
+        tt(T.e2[:], T.pn[:, 0:4], T.sy[:], ALU.mult, [("pn", 0, 256), "sy"], ["e2"])
+        q1("nd", "cnt", 0.5, ALU.is_lt)
+        q2("win", "nd", "pr", ALU.mult)
+        q2("w2", "w1", "win", ALU.mult)
+        q2("w3", "w2", "DM", ALU.add)
+        cp(T.offX[:], m("w3"), ["w3"], ["offX"])
+        tt(T.X[:].indirect(T.offX[:]), T.yk_[:], T.e2[:], ALU.add, ["yk_", "e2", "offX"], ["X"])
+        if last:
+            dma("y", [(T.yx[:], T.X[:, 0:4096], [], [("X", 0, 4096)])])
+        tt(T.nn[:], T.pe[:], T.xb[:], ALU.is_ge, ["pe", "xb"], ["nn"])
+        scan(T.fs[:], T.RSE[:], T.nn[:], ALU.add, ALU.min, ["RSE", "nn"], ["fs"])
+        tt(m("o1"), T.fs[:, 15::16], m("pr4"), ALU.mult, ["fs", "pr4"], ["o1"])
+        q2("o2", "o1", "bs2", ALU.add)
+        cp(T.offV[:], m("o2"), ["o2"], ["offV"])
+        for c in range(4):
+            tt(T.kp[:, c, :], T.KS[:].indirect(T.offV[:, 4 * c:4 * c + 4]), T.a1[:, 64 * c:64 * c + 64], ALU.add, ["KS", "offV", "a1"], [("kp", 64 * c, 64 * c + 64)])
+        dst = "kout" if last else "ku"
+        for rl in range(4):
+            cp(T[dst][:, :, :, rl], T.kp[:, :, 16 * rl:16 * rl + 16], ["kp"], [(dst, 64 * rl, 64 * rl + 64)])
+        if last:
+            dma("y", [(T.yk[:], T.kout[:], [], ["kout"])])
+        else:
+            send("ku", "kl%d" % (t + 1), nxt, "rk%d" % (t + 1), "lk%d" % (t + 1))
+        if not last:
+            op("v", lambda: g.vector.tensor_reduce(T.A1[:, 0:1], T.ps[:, 288:304], AxisListType.X, ALU.add), [("ps", 288, 304)], ["A1"])
+            tt(T.A[:, 0:1], T.A[:, 0:1], T.A1[:, 0:1], ALU.add, ["A", "A1"], ["A"])
+            cp(T.Ai[:, 0:1], T.A[:, 0:1], ["A"], [("Ai", 0, 1)])
+            ts(T.Ai[:, 1:2], T.Ai[:, 0:1], 15, ALU.bitwise_and, [("Ai", 0, 1)], [("Ai", 1, 2)])
+            ts(T.thr[:, 0:1], T.Ai[:, 1:2], 2.0, ALU.mult, [("Ai", 1, 2)], ["thr"], 520.0, ALU.add)
+    for sem in sorted(total):
+        if waited.get(("g", sem), 0) < total[sem]:
+            g.wait_ge(T.sem[sem], total[sem])

@@ -217,6 +217,7 @@ def rank_program(g, core, T, topo):
     for q in range(16):
         cp(T.SEL[:, q, q::16], T.BLK[:, q::16], ["BLK"], [("SEL", 128 * q, 128 * q + 128)])
     act(T.SELN[:], T.SEL[:], AF.Copy, ["SEL"], ["SELN"], scale=-0.5)
+    act(T.SELP[:], T.SEL[:], AF.Copy, ["SEL"], ["SELP"], scale=0.5)
     ts(T.ID[:], T.rowi[:], T.col[:, 0:1], ALU.is_equal, ["rowi", ("col", 0, 1)], ["ID"])
     ts(T.IDW[:], T.ID[:], 1.0 / 128, ALU.mult, ["ID"], ["IDW"])
     ts(T.IDN[:], T.ID[:], -1.0, ALU.mult, ["ID"], ["IDN"])
@@ -256,8 +257,6 @@ def rank_program(g, core, T, topo):
             a = 32 + 16 * i
             tt(T.pw2[:, 16 * i:16 * i + 16], T.pw2[:, a:a + 16], T.OH[:], ALU.mult, ["pw2", "OH"], ["pw2"])
             op("v", lambda i=i: g.vector.tensor_reduce(T.col[:, 5 + i:6 + i], T.pw2[:, 16 * i:16 * i + 16], AxisListType.X, ALU.add), ["pw2"], [("col", 5 + i, 6 + i)])
-        act(T.SELW[:], T.SEL[:], AF.Copy, ["SEL", ("col", 6, 7)], ["SELW"], scale=T.col[:, 6:7])
-        act(T.SELP[:], T.SEL[:], AF.Copy, ["SEL"], ["SELP"], scale=0.5)
         for rl in range(4):
             ts(T.col[:, 8 + rl:9 + rl], T.col[:, 7:8], float(rl), ALU.add, [("col", 7, 8)], [("col", 8 + rl, 9 + rl)])
         for rl in range(4):
@@ -355,6 +354,11 @@ def rank_program(g, core, T, topo):
         act(T.us[:, 0:192], T.ps[:, 0:192], AF.Copy, [("ps", 0, 192)], [("us", 0, 192)])
         mm(T.pk[:, 0:256], T.IDW[:], T.sg[:], False, True, ["IDW", "sg"], [("pk", 0, 256)])
         sgather(2)
+        if t == 0:
+            act(T.SELW[:], T.SEL[:], AF.Copy, ["SEL", ("col", 6, 7)], ["SELW"], scale=T.col[:, 6:7])
+        mm(T.pe[:], T.ID[:], T.Z0[:], True, False, ["ID", "Z0"], ["pe"])
+        for c in (3, 0, 1, 2):
+            pass_("pe", 64 * c, "SELN", "s%d" % c, False, False)
         tt(T.key[:], T.pk[:, 0:256], T.us[:], ALU.add, [("pk", 0, 256), "us"], ["key"])
         scan(T.R[:], T.RST[:], T.key[:], ALU.max, ALU.min, ["RST", "key"], ["R"])
         r = T.R[:, 15::16]
@@ -390,12 +394,10 @@ def rank_program(g, core, T, topo):
 
         spread(0, "k1b")
         spread(4, "f1b")
-        mm(T.pe[:], T.ID[:], T.Z0[:], True, False, ["ID", "Z0"], ["pe"])
 
         def second(c):
-            pass_("pe", 64 * c, "SELN", "s%d" % c, False, False)
-            for m in range(16):
-                tt(T["mx%d" % c][:, m::16], T["s%d" % c][:, m::16], T.px[:, c], ALU.max, ["s%d" % c, "px"], [("mx%d" % c, 64 * m, 64 * m + 64)])
+            for j in range(16):
+                tt(T["mx%d" % c][:, j::16], T["s%d" % c][:, j::16], T.px[:, c], ALU.max, ["s%d" % c, "px"], [("mx%d" % c, 64 * j, 64 * j + 64)])
             pass_("pe", 64 * c, "SEL", "mx%d" % c, False, c == 3)
 
         second(0)
@@ -457,7 +459,8 @@ def rank_program(g, core, T, topo):
         scan(T.xb[:], T.BC0[:], T.xz[:], ALU.mult, ALU.add, ["BC0", "xz"], ["xb"])
         q2("bs2", "bs", "CB", ALU.add)
         second(2)
-        second(3)
+        if not last:
+            second(3)
         ts(T.pn[:, 0:4], T.sw[:], 1.0, ALU.add, ["sw"], [("pn", 0, 256)], 64.0, ALU.mult)
         tt(m("w1"), T.ps[:, 272:288], T.DMH[:], ALU.subtract, [("ps", 272, 288), "DMH"], ["w1"])
         tt(T.e2[:], T.pn[:, 0:4], T.sy[:], ALU.mult, [("pn", 0, 256), "sy"], ["e2"])
@@ -469,6 +472,7 @@ def rank_program(g, core, T, topo):
         tt(T.X[:].indirect(T.offX[:]), T.yk_[:], T.e2[:], ALU.add, ["yk_", "e2", "offX"], ["X"])
         if last:
             dma("y", [(T.yx[:], T.X[:, 0:4096], [], [("X", 0, 4096)])])
+            second(3)
         tt(T.nn[:], T.pe[:], T.xb[:], ALU.is_ge, ["pe", "xb"], ["nn"])
         scan(T.fs[:], T.RSE[:], T.nn[:], ALU.add, ALU.min, ["RSE", "nn"], ["fs"])
         tt(m("o1"), T.fs[:, 15::16], m("pr4"), ALU.mult, ["fs", "pr4"], ["o1"])

from concourse.mybir import AluOpType as ALU, AxisListType, ActivationFunctionType as AF

BIG = 1.0e6
_B = "bfloat16"
_F = "float32"
_I = "int32"
_U = "uint16"
SCRATCH = {
    "X": ("sbuf", [128, 4352], _B),
    "KS": ("sbuf", [128, 4608], _F),
    "kd": ("dram", [8, 33, 256], _F),
    "kz": ("dram", [8, 4096], _F),
    "cm": ("sbuf", [128, 256], _F),
    "k15": ("sbuf", [128, 256], _F),
    "kin": ("sbuf", [128, 256], _I), "pin": ("sbuf", [128, 256], _I),
    "kl0": ("sbuf", [128, 256], _U), "kl1": ("sbuf", [128, 256], _U), "kl2": ("sbuf", [128, 256], _U),
    "pl0": ("sbuf", [128, 256], _U), "pl1": ("sbuf", [128, 256], _U), "pl2": ("sbuf", [128, 256], _U),
    "ku": ("sbuf", [128, 4, 16, 4], _U), "pu": ("sbuf", [128, 256], _U),
    "kout": ("sbuf", [128, 4, 16, 4], _F), "pout": ("sbuf", [128, 256], _F),
    "Pf": ("sbuf", [128, 256], _F), "P4": ("sbuf", [128, 256], _F),
    "t1": ("sbuf", [128, 256], _I), "t2": ("sbuf", [128, 256], _I),
    "pw": ("sbuf", [128, 256], _I), "px_": ("sbuf", [128, 256], _I),
    "pid": ("sbuf", [128, 4], _I), "row": ("sbuf", [128, 128], _I), "row2": ("sbuf", [128, 128], _I),
    "rowm": ("sbuf", [128, 128], _F), "rowi": ("sbuf", [128, 128], _F),
    "col": ("sbuf", [128, 16], _F), "r16": ("sbuf", [128, 16], _F), "OH": ("sbuf", [128, 16], _F),
    "GM": ("sbuf", [128, 8], _F), "pw2": ("sbuf", [128, 64], _F),
    "SEL": ("sbuf", [128, 16, 128], _B), "SELN": ("sbuf", [128, 16, 128], _B),
    "SELP": ("sbuf", [128, 16, 128], _B), "IDN": ("sbuf", [128, 128], _B),
    "SELW": ("sbuf", [128, 16, 128], _B), "SELT": ("sbuf", [128, 16, 128], _B),
    "BLK": ("sbuf", [128, 128], _B), "BLKF": ("sbuf", [128, 128], _F), "BLK0": ("sbuf", [128, 128], _F),
    "S15": ("sbuf", [128, 128], _F), "ID": ("sbuf", [128, 128], _B), "IDW": ("sbuf", [128, 128], _B),
    "JR": ("sbuf", [128, 256], _B), "JRF": ("sbuf", [128, 256], _F), "Z0": ("sbuf", [128, 256], _B),
    "RST": ("sbuf", [128, 256], _F), "RSE": ("sbuf", [128, 256], _F), "BC0": ("sbuf", [128, 256], _F),
    "C16": ("sbuf", [128, 16], _F), "CB": ("sbuf", [128, 16], _F), "DM": ("sbuf", [128, 16], _F),
    "DMH": ("sbuf", [128, 16], _F), "TRB": ("sbuf", [128, 4, 64], _B), "tri": ("sbuf", [128, 64], _F),
    "us": ("sbuf", [128, 256], _F), "key": ("sbuf", [128, 256], _F), "R": ("sbuf", [128, 256], _F), "sg": ("sbuf", [128, 256], _B),
    "sf": ("sbuf", [128, 384], _F), "si": ("sbuf", [128, 128], _I),
    "offF": ("sbuf", [128, 16], _U), "offK": ("sbuf", [128, 16], _U), "offV": ("sbuf", [128, 16], _U),
    "offX": ("sbuf", [128, 16], _U),
    "kill": ("sbuf", [128, 16], _B), "k1b": ("sbuf", [128, 16], _B), "f1b": ("sbuf", [128, 16], _B),
    "A": ("sbuf", [128, 4], _F), "A1": ("sbuf", [128, 4], _F), "Ai": ("sbuf", [128, 4], _I), "thr": ("sbuf", [128, 4], _F),
    "xn": ("sbuf", [128, 4, 64], _B), "xz": ("sbuf", [128, 256], _F), "xb": ("sbuf", [128, 256], _F),
    "nn": ("sbuf", [128, 256], _F), "fs": ("sbuf", [128, 256], _F), "a1": ("sbuf", [128, 256], _F),
    "kp": ("sbuf", [128, 4, 64], _F),
    "HPk": ("sbuf", [128, 4, 16, 4], _F), "HPf": ("sbuf", [128, 4, 16, 4], _F),
    "b1": ("sbuf", [128, 256], _I), "b2": ("sbuf", [128, 256], _I), "FB": ("sbuf", [128, 256], _B),
    "BD": ("sbuf", [128, 16, 8, 16], _B), "junk": ("sbuf", [128, 4096], _B),
    "ak": ("sbuf", [128, 256], _B), "yk_": ("sbuf", [128, 256], _B), "sw": ("sbuf", [128, 256], _B),
    "sy": ("sbuf", [128, 256], _B), "e2": ("sbuf", [128, 256], _B),
    "pk": ("psum", [128, 512], _F), "ps": ("psum", [128, 512], _F), "px": ("psum", [128, 4, 16, 4], _F),
    "pe": ("psum", [128, 256], _F), "pb": ("psum", [128, 8, 16, 4], _F), "pone": ("psum", [128, 512], _F),
    "pn": ("psum", [128, 8, 4, 16], _F), "pg": ("psum", [128, 512], _F),
}
for _c in range(4):
    for _n in ("y", "s", "d", "rl", "mx"):
        SCRATCH["%s%d" % (_n, _c)] = ("sbuf", [128, 1024], _B)
PSUM = ("pk", "ps", "px", "pe", "pb", "pone", "pn", "pg")
SEMAPHORES = ["qv", "qs", "qt", "qg"] + ["dm%d" % i for i in range(24)] + ["rk1", "rk2", "rp1", "rp2", "lk1", "lk2", "lp1", "lp2"]
ROUNDS = 3
SMF = ("w", "h1", "h2", "fo", "ko", "plt", "nk", "pr", "k1", "f1", "pr4", "bs", "bs2", "o1", "o2", "cnt", "nd", "win", "w1", "w2", "w3")
SMI = ("ki", "zm", "ub", "kk", "h3", "fi")


def rank_program(g, core, T, topo):
    rank = T.rank_of(core)
    if rank is None:
        return
    n_ranks = len(T.cores)
    eng = {"v": g.vector, "s": g.scalar, "t": g.tensor, "g": g, "y": g.sync}
    count = {"v": 0, "s": 0, "t": 0, "g": 0}
    total = {}
    waited = {}
    log = {}
    dmas = [0]

    def deps(q, reads, writes):
        need = {}
        for is_w, regs in ((False, reads), (True, writes)):
            for name, lo, hi in regs:
                bank = name in PSUM
                for (l, h, oq, sem, val, ow) in log.get(name, []):
                    if not bank and (h <= lo or hi <= l):
                        continue
                    if oq == q:
                        if q == "t" or (not ow):
                            continue
                        if is_w and bank and (h <= lo or hi <= l):
                            continue
                        if not is_w and (h <= lo or hi <= l):
                            continue
                    elif not bank and not ow and not is_w:
                        continue
                    if val > need.get(sem, 0):
                        need[sem] = val
        for sem in sorted(need):
            if waited.get((q, sem), 0) < need[sem]:
                waited[(q, sem)] = need[sem]
                eng[q].wait_ge(T.sem[sem], need[sem])

    def note(q, sem, val, reads, writes):
        for is_w, regs in ((False, reads), (True, writes)):
            for name, lo, hi in regs:
                old = log.get(name, [])
                if is_w:
                    old = [e for e in old if not (lo <= e[0] and e[1] <= hi)]
                else:
                    old = [e for e in old if not (e[2] == q and not e[5] and e[3] == sem and lo <= e[0] and e[1] <= hi)]
                old.append((lo, hi, q, sem, val, is_w))
                log[name] = old

    def m(name):
        if name in SMF:
            i = 16 * SMF.index(name)
            return T.sf[:, i:i + 16]
        if name in SMI:
            i = 16 * SMI.index(name)
            return T.si[:, i:i + 16]
        return T[name][:]

    def flat(name, lo=None, hi=None):
        if lo is None and (name in SMF or name in SMI):
            return (name, 0, 16)
        if lo is None:
            n = 1
            for x in SCRATCH[name][1][1:]:
                n *= x
            return (name, 0, n)
        return (name, lo, hi)

    def op(q, fn, reads, writes):
        reads = [flat(*r) if isinstance(r, tuple) else flat(r) for r in reads]
        writes = [flat(*r) if isinstance(r, tuple) else flat(r) for r in writes]
        deps(q, reads, writes)
        count[q] += 1
        sem = "q" + q
        total[sem] = count[q]
        fn().then_inc(T.sem[sem], 1)
        note(q, sem, count[q], reads, writes)

    def dma(q, pairs):
        sem = "dm%d" % dmas[0]
        dmas[0] += 1
        val = 16 * len(pairs)
        total[sem] = val
        done = []
        for out, in_, w, r in pairs:
            r = [flat(*x) if isinstance(x, tuple) else flat(x) for x in r]
            w = [flat(*x) if isinstance(x, tuple) else flat(x) for x in w]
            deps(q, r, w)
            eng[q].dma_start(out, in_).then_inc(T.sem[sem], 16)
            done.append((r, w))
        for r, w in done:
            note("dma", sem, val, r, [])
        for r, w in done:
            for x in w:
                log.setdefault(x[0], []).append((x[1], x[2], "dma", sem, val, True))

    def tt(out, a, b, o, reads, writes):
        op("v", lambda: g.vector.tensor_tensor(out, a, b, o), reads, writes)

    def ts(out, a, s1, o1, reads, writes, s2=None, o2=None):
        if o2 is None:
            op("v", lambda: g.vector.tensor_scalar(out, a, s1, None, o1), reads, writes)
        else:
            op("v", lambda: g.vector.tensor_scalar(out, a, s1, s2, o1, o2), reads, writes)

    def q1(out, a, s1, o1, s2=None, o2=None):
        ts(m(out), m(a), s1, o1, [a], [out], s2, o2)

    def q2(out, a, b, o):
        tt(m(out), m(a), m(b), o, [a, b], [out])

    def cp(out, a, reads, writes):
        op("v", lambda: g.vector.tensor_copy(out, a), reads, writes)

    def fill(name, c, ap=None):
        op("v", lambda: g.vector.memset(T[name][:] if ap is None else ap, c), [], [name])

    def act(out, a, f, reads, writes, **kw):
        op("s", lambda: g.scalar.activation(out, a, f, **kw), reads, writes)

    def mm(out, l, r, st, sp, reads, writes):
        op("t", lambda: g.tensor.matmul(out, l, r, st, sp), reads, writes)

    def scan(out, a, b, o1, o2, reads, writes):
        op("v", lambda: g.vector.tensor_tensor_scan(out, a, b, 0.0, o1, o2), reads, writes)

    def iota(name, ap, pat, base, mult):
        op("g", lambda: g.iota(ap, pat, base, mult, allow_small_or_imprecise_dtypes=True), [], [name])

    dma("y", [(T.pin[:], T.ph[:], ["pin"], [])])
    dma("y", [(T.kin[:], T.ka[:], ["kin"], [])])
    dma("y", [(T.X[:, 0:4096], T.x0[:], [("X", 0, 4096)], [])])
    iota("pid", T.pid[:, 0:1], [[0, 1]], 0, 1)
    iota("row", T.row[:], [[1, 128]], 0, 0)
    iota("r16", T.r16[:], [[1, 16]], 0, 0)
    iota("JRF", T.JRF[:], [[0, 16], [4, 16]], 1, 0)
    iota("C16", T.C16[:], [[0, 4], [16, 4]], 0, 0)
    iota("CB", T.CB[:], [[64, 4], [1, 4]], 0, 0)
    iota("DM", T.DM[:], [[16, 16]], 4096, 0)
    iota("tri", T.tri[:], [[1, 4], [4, 16]], 0, 0)
    fill("cm", -4096.0)
    dma("y", [(T.kz[:], T.cm[:], ["kz"], ["cm"]), (T.kd[:, 0, :], T.cm[0:8, :], [("kd", 0, 1)], ["cm"])])
    dma("y", [(T.KS[0::16, 0:4096], T.kz[:], [("KS", 0, 4096)], ["kz"])])
    fill("SEL", 0.0)
    ts(T.pid[:, 1:2], T.pid[:, 0:1], 15, ALU.bitwise_and, [("pid", 0, 1)], [("pid", 1, 2)])
    ts(T.pid[:, 2:3], T.pid[:, 0:1], 4, ALU.arith_shift_right, [("pid", 0, 1)], [("pid", 2, 3)])
    ts(T.row2[:], T.row[:], 4, ALU.arith_shift_right, ["row"], ["row2"])
    cp(T.rowi[:], T.row[:], ["row"], ["rowi"])
    cp(T.col[:, 0:3], T.pid[:, 0:3], [("pid", 0, 3)], [("col", 0, 3)])
    cp(T.rowm[:], T.row2[:], ["row2"], ["rowm"])
    ts(T.col[:, 3:4], T.col[:, 1:2], 1.0, ALU.add, [("col", 1, 2)], [("col", 3, 4)])
    ts(T.col[:, 4:5], T.col[:, 1:2], 64.0, ALU.mult, [("col", 1, 2)], [("col", 4, 5)])
    ts(T.col[:, 7:8], T.col[:, 1:2], 4.0, ALU.mult, [("col", 1, 2)], [("col", 7, 8)])
    ts(T.BLK[:], T.rowm[:], T.col[:, 2:3], ALU.is_equal, ["rowm", ("col", 2, 3)], ["BLK"])
    ts(T.OH[:], T.r16[:], T.col[:, 1:2], ALU.is_equal, ["r16", ("col", 1, 2)], ["OH"])
    for q in range(16):
        cp(T.SEL[:, q, q::16], T.BLK[:, q::16], ["BLK"], [("SEL", 128 * q, 128 * q + 128)])
    act(T.SELN[:], T.SEL[:], AF.Copy, ["SEL"], ["SELN"], scale=-0.5)
    act(T.SELP[:], T.SEL[:], AF.Copy, ["SEL"], ["SELP"], scale=0.5)
    ts(T.ID[:], T.rowi[:], T.col[:, 0:1], ALU.is_equal, ["rowi", ("col", 0, 1)], ["ID"])
    ts(T.IDW[:], T.ID[:], 1.0 / 128, ALU.mult, ["ID"], ["IDW"])
    ts(T.IDN[:], T.ID[:], -1.0, ALU.mult, ["ID"], ["IDN"])
    ts(T.JR[:], T.JRF[:], 1.0 / 128, ALU.mult, ["JRF"], ["JR"])
    cp(T.kl0[:], T.kin[:], ["kin"], ["kl0"])
    cp(T.pl0[:], T.pin[:], ["pin"], ["pl0"])
    fill("RST", -BIG)
    op("v", lambda: g.vector.memset(T.RST[:, 0::16], BIG), ["RST"], ["RST"])
    fill("thr", 520.0)
    fill("A", 0.0)
    ts(T.C16[:], T.C16[:], T.col[:, 4:5], ALU.add, ["C16", ("col", 4, 5)], ["C16"])
    ts(T.CB[:], T.CB[:], T.col[:, 7:8], ALU.add, ["CB", ("col", 7, 8)], ["CB"])
    ts(T.DM[:], T.DM[:], T.col[:, 1:2], ALU.add, ["DM", ("col", 1, 2)], ["DM"])
    ts(T.DMH[:], T.DM[:], -2047.5, ALU.add, ["DM"], ["DMH"])

    def constants2():
        for q in range(16):
            ts(T.SELT[:, q, :], T.BLK[:], T.OH[:, q:q + 1], ALU.mult, ["BLK", "OH"], [("SELT", 128 * q, 128 * q + 128)])
        cp(T.BLKF[:], T.BLK[:], ["BLK"], ["BLKF"])
        fill("BLK0", 0.0)
        op("v", lambda: g.vector.tensor_copy(T.BLK0[:, 0::16], T.BLK[:, 0::16]), ["BLK", "BLK0"], ["BLK0"])
        ts(T.S15[:], T.BLK[:], T.OH[:, 15:16], ALU.mult, ["BLK", "OH"], ["S15"])
        fill("Z0", 0.0)
        fill("RSE", -1.0 / 16)
        op("v", lambda: g.vector.memset(T.RSE[:, 0::16], BIG), ["RSE"], ["RSE"])
        fill("BC0", 1.0)
        op("v", lambda: g.vector.memset(T.BC0[:, 0::16], 0.0), ["BC0"], ["BC0"])
        fill("xz", 0.0)
        ts(T.GM[:], T.r16[:, 0:8], T.col[:, 2:3], ALU.is_equal, ["r16", ("col", 2, 3)], ["GM"])
        fill("pw2", 0.5, T.pw2[:, 0:16])
        fill("pw2", 2.0, T.pw2[:, 16:32])
        op("v", lambda: g.vector.tensor_tensor_scan(T.pw2[:, 32:48], T.pw2[:, 0:16], T.Z0[:, 0:16], 8192.0, ALU.mult, ALU.add), ["pw2", "Z0"], ["pw2"])
        op("v", lambda: g.vector.tensor_tensor_scan(T.pw2[:, 48:64], T.pw2[:, 16:32], T.Z0[:, 0:16], 0.25, ALU.mult, ALU.add), ["pw2", "Z0"], ["pw2"])
        op("v", lambda: g.vector.memset(T.pw2[:, 45:48], 0.0), ["pw2"], ["pw2"])
        op("v", lambda: g.vector.memset(T.pw2[:, 60:64], 0.0), ["pw2"], ["pw2"])
        for i in (0, 1):
            a = 32 + 16 * i
            tt(T.pw2[:, 16 * i:16 * i + 16], T.pw2[:, a:a + 16], T.OH[:], ALU.mult, ["pw2", "OH"], ["pw2"])
            op("v", lambda i=i: g.vector.tensor_reduce(T.col[:, 5 + i:6 + i], T.pw2[:, 16 * i:16 * i + 16], AxisListType.X, ALU.add), ["pw2"], [("col", 5 + i, 6 + i)])
        for rl in range(4):
            ts(T.col[:, 8 + rl:9 + rl], T.col[:, 7:8], float(rl), ALU.add, [("col", 7, 8)], [("col", 8 + rl, 9 + rl)])
        for rl in range(4):
            ts(T.TRB[:, rl, :], T.tri[:], T.col[:, 8 + rl:9 + rl], ALU.is_ge, ["tri", ("col", 8 + rl, 9 + rl)], [("TRB", 64 * rl, 64 * rl + 64)], -64.0, ALU.mult)

    def landed(name, sem, val):
        total[sem] = val
        log.setdefault(name, []).append((0, 256, "rem", sem, val, True))

    def send(name, land, dst, rs, ls):
        rid, pid, _ = topo.addr(dst)
        es = topo.engines(core, dst)[:8]
        mask = sum(1 << e for e in es)
        regs = [flat(name)]
        deps("g", regs, [])
        g.remote_dma(T[land][:], T[name][:], T.sem[rs], T.sem[ls], pid, rid, mask)
        total[ls] = len(es)
        note("rem", ls, len(es), regs, [])

    nxt = T.cores[(rank + 1) % n_ranks]
    prv = T.cores[(rank - 1) % n_ranks]
    KB = 17 * 256
    CN = 16 * SMF.index("cnt")

    for t in range(ROUNDS):
        last = t == ROUNDS - 1
        kl, pl = "kl%d" % t, "pl%d" % t
        KL, PL = T[kl], T[pl]
        if t:
            ne = len(topo.engines(core, nxt)[:8])
            landed(kl, "rk%d" % t, ne)
            landed(pl, "rp%d" % t, ne)
        if t == 0:
            fill("us", 0.0)
            constants2()
        cp(T.y0[:], T.X[:, 0:4096].indirect(PL[:, 0:64]), [("X", 0, 4096), pl], ["y0"])
        for c in (1, 2, 3):
            act(T["y%d" % c][:], T.X[:, 0:4096].indirect(PL[:, 64 * c:64 * c + 64]), AF.Copy, [("X", 0, 4096), pl], ["y%d" % c])
        cp(T.Pf[:], PL[:], [pl], ["Pf"])
        ts(T.P4[:], PL[:], 4096.0, ALU.add, [pl], ["P4"])
        cp(T.KS[:, KB:KB + 256], KL[:], [kl], [("KS", KB, KB + 256)])
        mm(T.pn[:, 0:4], T.S15[:], T.KS[:, KB:KB + 256], True, True, ["S15", ("KS", KB, KB + 256)], [("pn", 0, 256)])
        act(T["s3"][:], T.X[:, 0:4096].indirect(KL[:, 192:256]), AF.Copy, [("X", 0, 4096), kl], ["s3"])
        act(T.k15[:], T.pn[:, 0:4], AF.Copy, [("pn", 0, 256)], ["k15"])
        dma("y", [(T.kd[:, 1:17, :], T.KS[:, KB:KB + 256], [("kd", 1, 17)], [("KS", KB, KB + 256)]),
                  (T.kd[:, 17:33, :], T.k15[:], [("kd", 17, 33)], ["k15"])])
        dma("y", [(T.KS[j::16, 0:4096], T.kd[:, j + 1:j + 17, :], [("KS", 0, 4096)], [("kd", j + 1, j + 17)]) for j in range(1, 16)]
            + [(T.KS[:, 4096:KB], T.kd[:, 0:16, :], [("KS", 4096, KB)], [("kd", 0, 16)])])
        mm(T.pk[:, 0:256], T.ID[:], T.JR[:], True, False, ["ID", "JR"], [("pk", 0, 256)])

        def fused(c):
            tt(T["d%d" % c][:], T.X[:, 0:4096].indirect(KL[:, 64 * c:64 * c + 64]), T["y%d" % c][:], ALU.subtract, [("X", 0, 4096), kl, "y%d" % c], ["d%d" % c])

        def relu(c):
            ts(T["rl%d" % c][:], T["d%d" % c][:], 0.0, ALU.max, ["d%d" % c], ["rl%d" % c])

        def pass_(bank, lo, sel, src, first, final, rev=False):
            for q in range(16):
                mm(T[bank][:, lo:lo + 64], T[sel][:, q, :], T[src][:, 64 * q:64 * q + 64], first and q == 0, final and q == 15,
                   [sel, src], [(bank, lo, lo + 64)])

        def dpass(c):
            pass_("ps", 64 * c, "SELN", "d%d" % c, True, True)

        def rpass(c):
            pass_("pk", 64 * c, "SEL", "rl%d" % c, False, False)

        def sgather(c):
            act(T["s%d" % c][:], T.X[:, 0:4096].indirect(KL[:, 64 * c:64 * c + 64]), AF.Copy, [("X", 0, 4096), kl], ["s%d" % c])

        for h, bank in ((0, "pone"), (1, "pg")):
            mm(T[bank][:], T.ID[:], T.s3[:, 512 * h:512 * h + 512], True, False, ["ID", "s3"], [bank])
            mm(T[bank][:], T.IDN[:], T.y3[:, 512 * h:512 * h + 512], False, True, ["IDN", "y3"], [bank])
            act(T.rl3[:, 512 * h:512 * h + 512], T[bank][:], AF.Abs, [bank], [("rl3", 512 * h, 512 * h + 512)], scale=0.5)
        sgather(0)
        fused(0)
        relu(0)
        fused(1)
        dpass(0)
        rpass(0)
        pass_("ps", 192, "SELN", "s3", True, False)
        pass_("ps", 192, "SELP", "y3", False, True)
        rpass(3)
        relu(1)
        fused(2)
        dpass(1)
        rpass(1)
        relu(2)
        dpass(2)
        rpass(2)
        tt(T.t1[:], T.KS[:, KB:KB + 256], T.Pf[:], ALU.mult, [("KS", KB, KB + 256), "Pf"], ["t1"])
        ts(T.t2[:], T.t1[:], 5, ALU.arith_shift_right, ["t1"], ["t2"])
        sgather(1)
        act(T.sg[:], T.ps[:, 0:256], AF.Sign, [("ps", 0, 256)], ["sg"], scale=-1.0, bias=-0.25)
        act(T.us[:, 0:192], T.ps[:, 0:192], AF.Copy, [("ps", 0, 192)], [("us", 0, 192)])
        mm(T.pk[:, 0:256], T.IDW[:], T.sg[:], False, True, ["IDW", "sg"], [("pk", 0, 256)])
        sgather(2)
        if t == 0:
            act(T.SELW[:], T.SEL[:], AF.Copy, ["SEL", ("col", 6, 7)], ["SELW"], scale=T.col[:, 6:7])
        mm(T.pe[:], T.ID[:], T.Z0[:], True, False, ["ID", "Z0"], ["pe"])
        for c in (3, 0, 1, 2):
            pass_("pe", 64 * c, "SELN", "s%d" % c, False, False)
        tt(T.key[:], T.pk[:, 0:256], T.us[:], ALU.add, [("pk", 0, 256), "us"], ["key"])
        scan(T.R[:], T.RST[:], T.key[:], ALU.max, ALU.min, ["RST", "key"], ["R"])
        r = T.R[:, 15::16]
        ts(m("ki"), r, 64.0, ALU.mult, ["R"], ["ki"])
        ts(m("nk"), r, 440.0, ALU.is_ge, ["R"], ["nk"])
        ts(m("plt"), r, T.thr[:, 0:1], ALU.is_lt, ["R", "thr"], ["plt"])
        q1("ub", "ki", 1, ALU.bitwise_and)
        q1("zm", "ki", 5, ALU.arith_shift_right, 3, ALU.bitwise_and)
        q1("kk", "ki", 1, ALU.arith_shift_right, 15, ALU.bitwise_and)
        q1("w", "ub", 2.0, ALU.mult, -1.0, ALU.add)
        q2("pr", "plt", "nk", ALU.mult)
        q2("h2", "zm", "w", ALU.mult)
        q2("h1", "kk", "w", ALU.add)
        q2("h3", "h1", "h2", ALU.add)
        q1("fi", "h3", 15, ALU.bitwise_and)
        q2("fo", "fi", "C16", ALU.add)
        cp(T.offF[:], m("fo"), ["fo"], ["offF"])
        for c in range(4):
            cp(T.xn[:, c, :], T["y%d" % c][:].indirect(T.offF[:, 4 * c:4 * c + 4]), ["y%d" % c, "offF"], [("xn", 64 * c, 64 * c + 64)])
        for rl in range(4):
            mm(T.px[:, :, :, rl], T.ID[:], T.xn[:, :, 16 * rl:16 * rl + 16], True, True, ["ID", "xn"], ["px"])
        q1("k1", "kk", 1.0, ALU.add)
        q1("f1", "fi", 1.0, ALU.add)
        q2("ko", "kk", "C16", ALU.add)
        q2("k1b", "k1", "pr", ALU.mult)
        q2("f1b", "f1", "pr", ALU.mult)
        cp(T.offK[:], m("ko"), ["ko"], ["offK"])
        ts(T.kill[:], r, 440.0, ALU.is_lt, ["R"], ["kill"])

        def spread(b, src):
            for q in range(16):
                mm(T.pb[:, b:b + 4, q, :], T.SELT[:, q, :], T[src][:], True, True, ["SELT", src], [("pb", 64 * b, 64 * b + 256)])

        spread(0, "k1b")
        spread(4, "f1b")

        def second(c):
            for j in range(16):
                tt(T["mx%d" % c][:, j::16], T["s%d" % c][:, j::16], T.px[:, c], ALU.max, ["s%d" % c, "px"], [("mx%d" % c, 64 * j, 64 * j + 64)])
            pass_("pe", 64 * c, "SEL", "mx%d" % c, False, c == 3)

        second(0)
        ts(T.pone[:], T.pb[:], T.col[:, 3:4], ALU.is_equal, ["pb", ("col", 3, 4)], ["pone"])
        tt(T.HPk[:], T.pone[:, 0:256], T.P4[:], ALU.mult, [("pone", 0, 256), "P4"], ["HPk"])
        tt(T.HPf[:], T.pone[:, 256:512], T.P4[:], ALU.mult, [("pone", 256, 512), "P4"], ["HPf"])
        for rl in range(4):
            mm(T.pn[:, 0:4, rl, :], T.BLKF[:], T.HPk[:, :, :, rl], True, True, ["BLKF", "HPk"], [("pn", 0, 256)])
        for q in range(16):
            mm(T.ps[:, 256:272], T.SELN[:, q, :], T.xn[:, :, q::16], q == 0, q == 15, ["SELN", "xn"], [("ps", 256, 272)])
        spread(0, "kill")
        for c in range(4):
            src = "d%d" % c if c < 3 else "rl3"
            act(T.ak[:, 64 * c:64 * c + 64], T[src][:].indirect(T.offK[:, 4 * c:4 * c + 4]), AF.Abs, [src, "offK"], [("ak", 64 * c, 64 * c + 64)],
                scale=1.0 if c < 3 else 2.0)
        for c in range(4):
            act(T.yk_[:, 64 * c:64 * c + 64], T["y%d" % c][:].indirect(T.offK[:, 4 * c:4 * c + 4]), AF.Copy, ["y%d" % c, "offK"], [("yk_", 64 * c, 64 * c + 64)])
        act(T.sw[:], T.ak[:], AF.Sign, ["ak"], ["sw"], scale=-1.0, bias=32.5)
        act(T.sy[:], T.yk_[:], AF.Sign, ["yk_"], ["sy"], scale=-1.0, bias=127.5)
        second(1)
        ts(T.b1[:], T.pn[:, 0:4], T.col[:, 5:6], ALU.mult, [("pn", 0, 256), ("col", 5, 6)], ["b1"])
        ts(T.b2[:], T.b1[:], 4096, ALU.bitwise_and, ["b1"], ["b2"])
        ts(T.FB[:], T.b2[:], 1.0 / 2048, ALU.mult, ["b2"], ["FB"], -1.0, ALU.add)
        for i in range(8):
            ts(T.BD[:, :, i, :], T.FB[:], T.GM[:, i:i + 1], ALU.mult, ["FB", "GM"], [("BD", 256 * i, 256 * i + 256)])
        for rl in range(4):
            mm(T.pn[:, 4:8, rl, :], T.BLK0[:], T.HPf[:, :, :, rl], True, True, ["BLK0", "HPf"], [("pn", 256, 512)])
        act(T.a1[:], T.pn[:, 4:8], AF.Copy, [("pn", 256, 512)], ["a1"])
        for q in range(16):
            mm(T.ps[:, 272:288], T.SELW[:, q, :], T.FB[:, q::16], q == 0, q == 15, ["SELW", "FB"], [("ps", 272, 288)])
        mm(T.ps[:, 288:304], T.BLK[:], T.kill[:], True, True, ["BLK", "kill"], [("ps", 288, 304)])
        tt(T.pb[:, 4:8], T.t2[:], T.pb[:, 0:4], ALU.mult, ["t2", ("pb", 0, 256)], [("pb", 256, 512)])
        tt(T.pw[:], T.pb[:, 4:8], T.Pf[:], ALU.add, [("pb", 256, 512), "Pf"], ["pw"])
        ts(T.px_[:], T.pw[:], 4095, ALU.bitwise_and, ["pw"], ["px_"])
        if last:
            cp(T.pout[:], T.px_[:], ["px_"], ["pout"])
            dma("y", [(T.yp[:], T.pout[:], [], ["pout"])])
        else:
            cp(T.pu[:], T.px_[:], ["px_"], ["pu"])
            send("pu", "pl%d" % (t + 1), prv, "rp%d" % (t + 1), "lp%d" % (t + 1))
        for bank, rrs in (("pg", (12, 13)), ("pk", (14, 15)), ("pone", (8, 9)), ("pb", (10, 11)), ("pg", (4, 5, 6, 7)), ("pk", (0, 1, 2, 3))):
            lo = 0
            todo = []
            for rr in rrs:
                rh, rl = rr // 4, rr % 4
                n = 64 * (rh + 1)
                G = T[bank][:, lo // 64:(lo + n) // 64] if bank == "pb" else T[bank][:, lo:lo + n]
                mm(G, T.BD[:, rr, :, :], T.FB[:, 0:n], True, False, ["BD", "FB"], [(bank, lo, lo + n)])
                G2 = T[bank][:, (lo + n) // 64 - 1:(lo + n) // 64] if bank == "pb" else T[bank][:, lo + n - 64:lo + n]
                mm(G2, T.ID[:], T.TRB[:, rl, :], False, True, ["ID", "TRB"], [(bank, lo, lo + n)])
                todo.append((rr, n, lo, G))
                lo += n
            for rr, n, lo, G in todo:
                act(T.junk[:, 256 * rr:256 * rr + n], G, AF.Relu, [(bank, lo, lo + n)], [("cnt", rr, rr + 1), ("junk", 256 * rr, 256 * rr + n)], bias=-15.0,
                    accum_out=T.sf[:, CN + rr:CN + rr + 1])
        ts(T.xz[:, 0::16], T.ps[:, 256:272], -1.0, ALU.mult, [("ps", 256, 272)], ["xz"], 480.0, ALU.add)
        q1("pr4", "pr", 4096.0, ALU.mult)
        q1("bs", "pr", -512.0, ALU.mult, 4352.0, ALU.add)
        scan(T.xb[:], T.BC0[:], T.xz[:], ALU.mult, ALU.add, ["BC0", "xz"], ["xb"])
        q2("bs2", "bs", "CB", ALU.add)
        second(2)
        if not last:
            second(3)
        ts(T.pn[:, 0:4], T.sw[:], 1.0, ALU.add, ["sw"], [("pn", 0, 256)], 64.0, ALU.mult)
        tt(m("w1"), T.ps[:, 272:288], T.DMH[:], ALU.subtract, [("ps", 272, 288), "DMH"], ["w1"])
        tt(T.e2[:], T.pn[:, 0:4], T.sy[:], ALU.mult, [("pn", 0, 256), "sy"], ["e2"])
        q1("nd", "cnt", 0.5, ALU.is_lt)
        q2("win", "nd", "pr", ALU.mult)
        q2("w2", "w1", "win", ALU.mult)
        q2("w3", "w2", "DM", ALU.add)
        cp(T.offX[:], m("w3"), ["w3"], ["offX"])
        tt(T.X[:].indirect(T.offX[:]), T.yk_[:], T.e2[:], ALU.add, ["yk_", "e2", "offX"], ["X"])
        if last:
            dma("y", [(T.yx[:], T.X[:, 0:4096], [], [("X", 0, 4096)])])
            second(3)
        tt(T.nn[:], T.pe[:], T.xb[:], ALU.is_ge, ["pe", "xb"], ["nn"])
        scan(T.fs[:], T.RSE[:], T.nn[:], ALU.add, ALU.min, ["RSE", "nn"], ["fs"])
        tt(m("o1"), T.fs[:, 15::16], m("pr4"), ALU.mult, ["fs", "pr4"], ["o1"])
        q2("o2", "o1", "bs2", ALU.add)
        cp(T.offV[:], m("o2"), ["o2"], ["offV"])
        for c in range(4):
            tt(T.kp[:, c, :], T.KS[:].indirect(T.offV[:, 4 * c:4 * c + 4]), T.a1[:, 64 * c:64 * c + 64], ALU.add, ["KS", "offV", "a1"], [("kp", 64 * c, 64 * c + 64)])
        dst = "kout" if last else "ku"
        for rl in range(4):
            cp(T[dst][:, :, :, rl], T.kp[:, :, 16 * rl:16 * rl + 16], ["kp"], [(dst, 64 * rl, 64 * rl + 64)])
        if last:
            dma("y", [(T.yk[:], T.kout[:], [], ["kout"])])
        else:
            send("ku", "kl%d" % (t + 1), nxt, "rk%d" % (t + 1), "lk%d" % (t + 1))
        if not last:
            op("v", lambda: g.vector.tensor_reduce(T.A1[:, 0:1], T.ps[:, 288:304], AxisListType.X, ALU.add), [("ps", 288, 304)], ["A1"])
            tt(T.A[:, 0:1], T.A[:, 0:1], T.A1[:, 0:1], ALU.add, ["A", "A1"], ["A"])
            cp(T.Ai[:, 0:1], T.A[:, 0:1], ["A"], [("Ai", 0, 1)])
            ts(T.Ai[:, 1:2], T.Ai[:, 0:1], 15, ALU.bitwise_and, [("Ai", 0, 1)], [("Ai", 1, 2)])
            ts(T.thr[:, 0:1], T.Ai[:, 1:2], 2.0, ALU.mult, [("Ai", 1, 2)], ["thr"], 520.0, ALU.add)
    for sem in sorted(total):
        if waited.get(("g", sem), 0) < total[sem]:
            g.wait_ge(T.sem[sem], total[sem])
